import numpy as np
import ml_dtypes


def mxq(x, axis, fmt="e4m3"):
    dtype, down = {"e4m3": (ml_dtypes.float8_e4m3fn, 7), "e5m2": (ml_dtypes.float8_e5m2, 14)}[fmt]
    v = np.moveaxis(np.asarray(x, np.float32).astype(ml_dtypes.bfloat16).astype(np.float64), axis, -1)
    blocks = v.reshape(v.shape[:-1] + (-1, 32))
    amax = np.abs(blocks).max(-1, keepdims=True)
    byte = np.maximum(np.where(amax > 0, np.frexp(amax)[1] - 1 + 127, 0) - down, 1)
    scale = np.exp2(byte - 127.0)
    codes = (blocks / scale).astype(np.float32).astype(dtype).astype(np.float64)
    return np.moveaxis((codes * scale).reshape(v.shape), -1, axis)


WIDE = False


def mx_kscale(k):
    if not WIDE:
        return np.ones(k)
    levels = np.array([30, -30])
    if k % 512:
        return np.exp2(np.random.permutation(np.resize(levels, k // 32))).repeat(32)
    a = np.empty((k // 512, 16))
    for p in range(k // 512):
        a[p, :8] = np.random.permutation(np.resize(levels, 8))
        for g in range(8):
            far = levels[np.abs(levels - a[p, g]) >= 10]
            a[p, g + 8] = far[np.random.randint(len(far))]
    return np.exp2(a.ravel()).repeat(32)


def f64(x):
    return np.asarray(x).astype(np.float64)


def striped(idx):
    return np.tile(np.asarray(idx).reshape(-1, 16).T, (8, 1)).astype(np.uint16)


def unstriped(offs):
    return offs[:16].T.reshape(-1).astype(np.int64)


E2M1 = np.array([0.0, 0.5, 1.0, 1.5, 2.0, 3.0, 4.0, 6.0, -0.0, -0.5, -1.0, -1.5, -2.0, -3.0, -4.0, -6.0])


def pack_weight(w, fmt):
    k, n = w.shape
    w = f64(np.asarray(w, np.float32).astype(ml_dtypes.bfloat16)).reshape(k // 32, 32, n)
    amax = np.abs(w).max(1)
    if fmt in ("e4m3", "e5m2"):
        byte = np.frexp(amax)[1] - 1 + 127 - (7 if fmt == "e4m3" else 14)
    else:
        mant, ex = np.frexp(amax / 6.0)
        byte = np.where(mant > 0.5, ex, ex - 1) + 127
    byte = np.clip(np.where(amax > 0, byte, 1), 1, 254)
    scaled = (w * np.exp2(127.0 - byte)[:, None, :]).reshape(k, n).astype(np.float32)
    by_word = np.ascontiguousarray(scaled.reshape(k // 512, 128, 4, n).transpose(0, 1, 3, 2))
    if fmt in ("e4m3", "e5m2"):
        words = by_word.astype(ml_dtypes.float8_e4m3fn if fmt == "e4m3" else ml_dtypes.float8_e5m2).view(np.uint8)
    else:
        c = by_word.astype(ml_dtypes.float4_e2m1fn).view(np.uint8) & 0xF
        words = (c[..., 0::2] | (c[..., 1::2] << 4)).reshape(k // 512, 128, 2 * n)
    return np.ascontiguousarray(words), np.ascontiguousarray(byte.astype(np.uint8).reshape(k // 512, 16, n))


def unpack_weight(words, scales, fmt):
    g, _, n = scales.shape
    words = np.ascontiguousarray(words).reshape(g, 128, n, -1)
    if fmt in ("e4m3", "e5m2"):
        vals = words.view(ml_dtypes.float8_e4m3fn if fmt == "e4m3" else ml_dtypes.float8_e5m2).astype(np.float64)
    else:
        nib = np.empty((g, 128, n, 4), np.uint8)
        nib[..., 0::2] = words & 0xF
        nib[..., 1::2] = words >> 4
        vals = E2M1[nib]
    vals = vals * np.repeat(np.exp2(scales.astype(np.float64) - 127.0), 8, axis=1)[..., None]
    return vals.transpose(0, 1, 3, 2).reshape(g * 512, n)


def sgn(shape):
    return np.random.uniform(0.5, 2.0, shape) * np.where(np.random.standard_normal(shape) < 0, -1.0, 1.0)


K, T, J, R, V, C, X, O, N, U, E = 512, 1024, 256, 512, 1024, 512, 1024, 256, 256, 128, 512


def setup_inputs():
    n = np.random.standard_normal
    idx = np.random.permutation(V)[:R]
    idx2 = np.random.permutation(T)[:J]
    idx3 = np.random.permutation(C)[:J]
    idx4 = np.random.permutation(X)[:C]
    idx5 = np.random.permutation(C)[:O]
    idx6 = np.random.permutation(O)[:U]
    idx7 = np.random.permutation(E)[:U]
    fk = mx_kscale(K)
    fr = mx_kscale(R)
    tr = np.ones(V)
    tr[idx] = fr
    xtp = pack_weight(n((K, T)) / fk[:, None], "e5m2")
    wtp = pack_weight(n((K, V)) * 1 / np.sqrt(K) * fk[:, None] * tr, "e2m1")
    wbp = pack_weight(n((R, N)) * 1 / np.sqrt(R) / fr[:, None], "e2m1")
    return {
        "xt_words": xtp[0],
        "xt_scales": xtp[1],
        "wt_words": wtp[0],
        "wt_scales": wtp[1],
        "tb": (n((R, X)) * 0.9).astype(np.float32),
        "wb_words": wbp[0],
        "wb_scales": wbp[1],
        "so": (sgn((N, 1))).astype(np.float32),
        "offs": striped(idx),
        "offs2": striped(idx2),
        "offs3": striped(idx3),
        "offs4": striped(idx4),
        "offs5": striped(idx5),
        "offs6": striped(idx6),
        "offs7": striped(idx7),
    }


def reference(xt_words, xt_scales, wt_words, wt_scales, tb, wb_words, wb_scales, so, offs, offs2, offs3, offs4, offs5, offs6, offs7):
    idx = unstriped(offs)
    idx2 = unstriped(offs2)
    idx3 = unstriped(offs3)
    idx4 = unstriped(offs4)
    idx5 = unstriped(offs5)
    idx6 = unstriped(offs6)
    idx7 = unstriped(offs7)
    xtu = unpack_weight(xt_words, xt_scales, "e5m2")
    wtu = unpack_weight(wt_words, wt_scales, "e2m1")
    wbu = unpack_weight(wb_words, wb_scales, "e2m1")
    wtidxg = wtu[:, idx]
    xtidx2g = xtu[:, idx2]
    a = wtidxg.T @ xtidx2g
    la = a[:, 0:1]
    pw = np.zeros((R, C))
    pw[:, idx3] = a
    pg = np.abs(pw - f64(tb)[:, idx4] * la)
    hid = pg[:, idx5]
    hidq = mxq(hid, 0, "e4m3")
    p = wbu.T @ hidq
    m0 = p[:, idx6] * f64(so)
    y = np.zeros((N, E))
    y[:, idx7] = m0
    return y

@@ -1,0 +1,161 @@
+from contextlib import ExitStack
+
+import concourse.mybir as mybir
+
+K, T, J, R, V, C, X, O, N, U, E = 512, 1024, 256, 512, 1024, 512, 1024, 256, 256, 128, 512
+FLOPS = 2 * K * R * J + 2 * R * N * O
+
+F32 = mybir.dt.float32
+BF16 = mybir.dt.bfloat16
+I32 = mybir.dt.int32
+U32 = mybir.dt.uint32
+U16 = mybir.dt.uint16
+U8 = mybir.dt.uint8
+E4M3X4 = mybir.dt.float8_e4m3fn_x4
+E5M2X4 = mybir.dt.float8_e5m2_x4
+E2M1X4 = mybir.dt.float4_e2m1fn_x4
+ACT = mybir.ActivationFunctionType
+ALU = mybir.AluOpType
+
+P = 128
+PACK = 4
+HALVES = N // P
+
+
+def load_list(nc, pool, offs, name):
+    tile = pool.tile(list(offs.shape), U16, name=name)
+    nc.sync.dma_start(tile[:], offs)
+    return tile
+
+
+def load_scale_rows(queue, plane, scales):
+    for q in range(4):
+        queue.dma_start(plane[32 * q : 32 * q + 4, :].bitcast(I32), scales[0, 4 * q : 4 * q + 4, :].bitcast(I32))
+
+
+def copy_on(nc, engine, out, in_):
+    if engine == "V":
+        nc.vector.tensor_copy(out, in_)
+    else:
+        nc.scalar.activation(out, in_, ACT.Copy)
+
+
+def tile_list_stamplead_chosen_one_postedout_kernel(
+    tc, xt_words, xt_scales, wt_words, wt_scales, tb, wb_words, wb_scales, so,
+    offs, offs2, offs3, offs4, offs5, offs6, offs7, out,
+):
+    nc = tc.nc
+    with ExitStack() as ctx:
+        keep = ctx.enter_context(tc.tile_pool(name="keep", bufs=1))
+        psum = ctx.enter_context(tc.psum_pool(name="psum", bufs=1))
+
+        wt_plane = keep.tile([P, V], U8, align_bytes=64)
+        xt_plane = keep.tile([P, T], U8, align_bytes=64)
+        wb_plane = keep.tile([P, N], U8, align_bytes=64)
+        for plane in (wt_plane, xt_plane, wb_plane):
+            nc.vector.memset(plane[:].bitcast(I32), 0)
+        pw = [keep.tile([P, C], F32, name=f"pw{t}") for t in range(PACK)]
+        page = [keep.tile([P, E], F32, name=f"page{h}") for h in range(HALVES)]
+        for tile in pw[:2]:
+            nc.vector.memset(tile[:], 0.0)
+        for tile in pw[2:] + page:
+            nc.gpsimd.memset(tile[:], 0.0)
+
+        idx = load_list(nc, keep, offs, "idx")
+        wt_tab = keep.tile([P, V], U16, align_bytes=64)
+        nc.sync.dma_start(wt_tab[:].bitcast(I32), wt_words[0].bitcast(I32))
+        load_scale_rows(nc.sync, wt_plane, wt_scales)
+        idx2 = load_list(nc, keep, offs2, "idx2")
+        xt_tab = keep.tile([P, T], I32, align_bytes=64)
+        nc.sync.dma_start(xt_tab[:], xt_words[0].rearrange("p c r -> p (c r)").bitcast(I32))
+        load_scale_rows(nc.sync, xt_plane, xt_scales)
+        idx4 = load_list(nc, keep, offs4, "idx4")
+        idx3 = load_list(nc, keep, offs3, "idx3")
+        tb_rows = tb.rearrange("(p t) x -> t p x", t=PACK)
+        tb_tab = [keep.tile([P, X], F32, name=f"tb{t}") for t in range(PACK)]
+        for t in range(PACK):
+            nc.sync.dma_start(tb_tab[t][:], tb_rows[t])
+        idx5 = load_list(nc, keep, offs5, "idx5")
+        wb_codes = keep.tile([P, 2 * N], U8, align_bytes=64)
+        nc.sync.dma_start(wb_codes[:].bitcast(I32), wb_words[0].bitcast(I32))
+        load_scale_rows(nc.sync, wb_plane, wb_scales)
+        idx6 = load_list(nc, keep, offs6, "idx6")
+        idx7 = load_list(nc, keep, offs7, "idx7")
+        so_cols = keep.tile([P, HALVES], F32)
+        with nc.allow_non_contiguous_dma(reason="one weight a partition for each half of the output features"):
+            nc.sync.dma_start(so_cols[:], so.rearrange("(h p) o -> p (h o)", p=P))
+
+        wt_picked = keep.tile([P, R], U16, align_bytes=64)
+        nc.vector.tensor_copy(wt_picked[:], wt_tab[:].indirect(idx[:]))
+        wt_sc = keep.tile([P, R], U8, align_bytes=64)
+        nc.vector.tensor_copy(wt_sc[:].rearrange("p (t m) -> p m t", t=PACK), wt_plane[:].indirect(idx[:]))
+        wt_dealt = keep.tile([P, R], U16, align_bytes=64)
+        nc.vector.tensor_copy(
+            wt_dealt[:].rearrange("p (t m) -> p t m", t=PACK), wt_picked[:].rearrange("p (m t) -> p t m", t=PACK)
+        )
+        xt_picked = keep.tile([P, J], U32, align_bytes=64)
+        nc.vector.tensor_copy(xt_picked[:], xt_tab[:].bitcast(U32).indirect(idx2[:]))
+        xt_sc = keep.tile([P, J], U8, align_bytes=64)
+        nc.vector.tensor_copy(xt_sc[:], xt_plane[:].indirect(idx2[:]))
+
+        a_psum = [psum.tile([P, J], F32, name=f"a_psum{t}") for t in range(PACK)]
+        for t in range(PACK):
+            nc.tensor.matmul_mx(
+                out=a_psum[t][:],
+                lhsT=wt_dealt[:, t * P : (t + 1) * P].bitcast(E2M1X4),
+                lhsT_scale=wt_sc[:, t * P : (t + 1) * P],
+                rhs=xt_picked[:].bitcast(E5M2X4),
+                rhs_scale=xt_sc[:],
+                start=True,
+                stop=True,
+            )
+
+        a = [keep.tile([P, J], F32, name=f"a{t}", tag="a_last_then_pg" if t == PACK - 1 else f"a{t}") for t in range(PACK)]
+        based = [keep.tile([P, C], F32, name=f"based{t}") for t in range(PACK)]
+        diff = [keep.tile([P, C], F32, name=f"diff{t}") for t in range(PACK)]
+        picked = keep.tile([P, PACK, O], F32)
+        hid = keep.tile([P, O, PACK], BF16, align_bytes=64)
+        last = PACK - 1
+        for t in range(PACK):
+            copy_on(nc, "SV"[t % 2], a[t][:], a_psum[t][:])
+        for t in range(PACK):
+            nc.scalar.activation(based[t][:], tb_tab[t][:].indirect(idx4[:]), ACT.Copy, scale=a[t][:, 0:1])
+            copy_on(nc, "S" if t == last else "V", pw[t][:].indirect(idx3[:]), a[t][:])
+        for t in range(PACK):
+            nc.vector.tensor_tensor(diff[t][:], pw[t][:], based[t][:], ALU.subtract)
+        pg = keep.tile([P, PACK, C], F32, tag="a_last_then_pg")
+        for t in range(PACK):
+            if t == last:
+                nc.vector.scalar_tensor_tensor(pg[:, t, :], diff[t][:], -1.0, diff[t][:], ALU.mult, ALU.max)
+            else:
+                nc.scalar.activation(pg[:, t, :], diff[t][:], ACT.Abs)
+        for t in range(PACK):
+            copy_on(nc, "SSVV"[t], picked[:, t, :], pg[:, t, :].indirect(idx5[:]))
+        nc.vector.tensor_copy(
+            hid[:].rearrange("p (c i) t -> p c t i", i=4), picked[:].rearrange("p t (c i) -> p c t i", i=4)
+        )
+
+        hid_codes = keep.tile([P, O], U32, align_bytes=64)
+        hid_sc = keep.tile([P, O], U8, align_bytes=64)
+        nc.vector.quantize_mx(
+            out=hid_codes[:].bitcast(E4M3X4), scales=hid_sc[:], in_=hid[:].rearrange("p o t -> p (o t)")
+        )
+        p_rows = [keep.tile([P, O], F32, name=f"p_rows{h}") for h in range(HALVES)]
+        ends = [keep.tile([P, U], F32, name=f"ends{h}") for h in range(HALVES)]
+        for h in range(HALVES):
+            p_psum = psum.tile([P, O], F32, name=f"p_psum{h}")
+            nc.tensor.matmul_mx(
+                out=p_psum[:],
+                lhsT=wb_codes[:, 2 * h * P : 2 * (h + 1) * P].bitcast(E2M1X4),
+                lhsT_scale=wb_plane[:, h * P : (h + 1) * P],
+                rhs=hid_codes[:].bitcast(E4M3X4),
+                rhs_scale=hid_sc[:],
+                start=True,
+                stop=True,
+            )
+            copy_on(nc, "SV"[h], p_rows[h][:], p_psum[:])
+        for h in range(HALVES):
+            nc.scalar.activation(ends[h][:], p_rows[h][:].indirect(idx6[:]), ACT.Copy, scale=so_cols[:, h : h + 1])
+        for h, queue in enumerate((nc.sync, nc.scalar)):
+            copy_on(nc, "VS"[h], page[h][:].indirect(idx7[:]), ends[h][:])
+            queue.dma_start(out[h * P : (h + 1) * P, :], page[h][:])

@@ -72,7 +72,7 @@ def tile_list_stamplead_chosen_one_postedout_kernel(
         idx4 = load_list(nc, keep, offs4, "idx4")
         idx3 = load_list(nc, keep, offs3, "idx3")
         tb_rows = tb.rearrange("(p t) x -> t p x", t=PACK)
-        tb_tab = [keep.tile([P, X], F32, name=f"tb{t}") for t in range(PACK)]
+        tb_tab = [keep.tile([P, X], F32, name=f"tb{t}", tag="tb_last_then_pg" if t == PACK - 1 else f"tb{t}") for t in range(PACK)]
         for t in range(PACK):
             nc.sync.dma_start(tb_tab[t][:], tb_rows[t])
         idx5 = load_list(nc, keep, offs5, "idx5")
@@ -110,50 +110,76 @@ def tile_list_stamplead_chosen_one_postedout_kernel(
                 stop=True,
             )
 
-        a = [keep.tile([P, J], F32, name=f"a{t}", tag="a_last_then_pg" if t == PACK - 1 else f"a{t}") for t in range(PACK)]
+        a = keep.tile([P, PACK, J], F32)
+        for t in range(PACK):
+            copy_on(nc, "V" if t == 0 else "S", a[:, t, :], a_psum[t][:])
+
         based = [keep.tile([P, C], F32, name=f"based{t}") for t in range(PACK)]
-        diff = [keep.tile([P, C], F32, name=f"diff{t}") for t in range(PACK)]
+        diff = [keep.tile([P, C], F32, name=f"diff{t}", tag=f"diff{t}") for t in range(PACK)]
+        pg = {}
         picked = keep.tile([P, PACK, O], F32)
         hid = keep.tile([P, O, PACK], BF16, align_bytes=64)
-        last = PACK - 1
-        for t in range(PACK):
-            copy_on(nc, "SV"[t % 2], a[t][:], a_psum[t][:])
-        for t in range(PACK):
-            nc.scalar.activation(based[t][:], tb_tab[t][:].indirect(idx4[:]), ACT.Copy, scale=a[t][:, 0:1])
-            copy_on(nc, "S" if t == last else "V", pw[t][:].indirect(idx3[:]), a[t][:])
-        for t in range(PACK):
-            nc.vector.tensor_tensor(diff[t][:], pw[t][:], based[t][:], ALU.subtract)
-        pg = keep.tile([P, PACK, C], F32, tag="a_last_then_pg")
-        for t in range(PACK):
-            if t == last:
-                nc.vector.scalar_tensor_tensor(pg[:, t, :], diff[t][:], -1.0, diff[t][:], ALU.mult, ALU.max)
-            else:
-                nc.scalar.activation(pg[:, t, :], diff[t][:], ACT.Abs)
-        for t in range(PACK):
-            copy_on(nc, "SSVV"[t], picked[:, t, :], pg[:, t, :].indirect(idx5[:]))
-        nc.vector.tensor_copy(
-            hid[:].rearrange("p (c i) t -> p c t i", i=4), picked[:].rearrange("p t (c i) -> p c t i", i=4)
-        )
 
-        hid_codes = keep.tile([P, O], U32, align_bytes=64)
-        hid_sc = keep.tile([P, O], U8, align_bytes=64)
-        nc.vector.quantize_mx(
-            out=hid_codes[:].bitcast(E4M3X4), scales=hid_sc[:], in_=hid[:].rearrange("p o t -> p (o t)")
-        )
+        def fetch_base(t):
+            nc.scalar.activation(based[t][:], tb_tab[t][:].indirect(idx4[:]), ACT.Copy, scale=a[:, t, 0:1])
+
+        def put(t, engine):
+            copy_on(nc, engine, pw[t][:].indirect(idx3[:]), a[:, t, :])
+
+        def subtract(t, engine):
+            engine.tensor_tensor(diff[t][:], pw[t][:], based[t][:], ALU.subtract)
+
+        def magnitude(t):
+            nc.scalar.activation(pg[t], diff[t][:], ACT.Abs)
+
+        def pick(t, engine):
+            copy_on(nc, engine, picked[:, t, :], pg[t].indirect(idx5[:]))
+
+        def weave(ts, cols):
+            nc.vector.tensor_copy(hid[:, cols, ts], picked[:, ts, cols].rearrange("p t o -> p o t"))
+
+        for t in range(PACK):
+            fetch_base(t)
+            put(t, "V")
+            subtract(t, nc.vector if t == 3 else nc.gpsimd)
+        pg_front = keep.tile([P, 3, C], F32, tag="tb_last_then_pg")
+        for t in range(3):
+            pg[t] = pg_front[:, t, :]
+        magnitude(0)
+        magnitude(1)
+        pick(0, "S")
+        magnitude(2)
+        pg_last = keep.tile([P, C], F32, tag="diff2")
+        pg[3] = pg_last[:]
+        magnitude(3)
+        pick(3, "S")
+        pick(1, "V")
+        pick(2, "V")
+        weave(slice(0, 2), slice(0, O))
+        places = O // 2
         p_rows = [keep.tile([P, O], F32, name=f"p_rows{h}") for h in range(HALVES)]
         ends = [keep.tile([P, U], F32, name=f"ends{h}") for h in range(HALVES)]
-        for h in range(HALVES):
-            p_psum = psum.tile([P, O], F32, name=f"p_psum{h}")
-            nc.tensor.matmul_mx(
-                out=p_psum[:],
-                lhsT=wb_codes[:, 2 * h * P : 2 * (h + 1) * P].bitcast(E2M1X4),
-                lhsT_scale=wb_plane[:, h * P : (h + 1) * P],
-                rhs=hid_codes[:].bitcast(E4M3X4),
-                rhs_scale=hid_sc[:],
-                start=True,
-                stop=True,
+        for s in range(2):
+            weave(slice(2, 4), slice(s * places, (s + 1) * places))
+        for s in range(2):
+            cols = slice(s * places, (s + 1) * places)
+            hid_codes = keep.tile([P, places], U32, name=f"hid_codes{s}", align_bytes=64)
+            hid_sc = keep.tile([P, places], U8, name=f"hid_sc{s}", align_bytes=64)
+            nc.vector.quantize_mx(
+                out=hid_codes[:].bitcast(E4M3X4), scales=hid_sc[:], in_=hid[:, cols, :].rearrange("p o t -> p (o t)")
             )
-            copy_on(nc, "SV"[h], p_rows[h][:], p_psum[:])
+            for h in range(HALVES):
+                p_psum = psum.tile([P, places], F32, name=f"p_psum{s}{h}")
+                nc.tensor.matmul_mx(
+                    out=p_psum[:],
+                    lhsT=wb_codes[:, 2 * h * P : 2 * (h + 1) * P].bitcast(E2M1X4),
+                    lhsT_scale=wb_plane[:, h * P : (h + 1) * P],
+                    rhs=hid_codes[:].bitcast(E4M3X4),
+                    rhs_scale=hid_sc[:],
+                    start=True,
+                    stop=True,
+                )
+                copy_on(nc, "V" if (s, h) == (1, 0) else "S", p_rows[h][:, cols], p_psum[:])
         for h in range(HALVES):
             nc.scalar.activation(ends[h][:], p_rows[h][:].indirect(idx6[:]), ACT.Copy, scale=so_cols[:, h : h + 1])
         for h, queue in enumerate((nc.sync, nc.scalar)):

@@ -50,7 +50,7 @@ def tile_list_stamplead_chosen_one_postedout_kernel(
         psum = ctx.enter_context(tc.psum_pool(name="psum", bufs=1))
 
         wt_plane = keep.tile([P, V], U8, align_bytes=64)
-        xt_plane = keep.tile([P, T], U8, align_bytes=64)
+        xt_plane = keep.tile([P, T], U8, align_bytes=64, tag="xt_plane_then_dealt")
         wb_plane = keep.tile([P, N], U8, align_bytes=64)
         for plane in (wt_plane, xt_plane, wb_plane):
             nc.vector.memset(plane[:].bitcast(I32), 0)
@@ -72,7 +72,7 @@ def tile_list_stamplead_chosen_one_postedout_kernel(
         idx4 = load_list(nc, keep, offs4, "idx4")
         idx3 = load_list(nc, keep, offs3, "idx3")
         tb_rows = tb.rearrange("(p t) x -> t p x", t=PACK)
-        tb_tab = [keep.tile([P, X], F32, name=f"tb{t}", tag="tb_last_then_pg" if t == PACK - 1 else f"tb{t}") for t in range(PACK)]
+        tb_tab = [keep.tile([P, X], F32, name=f"tb{t}", tag=f"tb{t}") for t in range(PACK)]
         for t in range(PACK):
             nc.sync.dma_start(tb_tab[t][:], tb_rows[t])
         idx5 = load_list(nc, keep, offs5, "idx5")
@@ -89,30 +89,42 @@ def tile_list_stamplead_chosen_one_postedout_kernel(
         nc.vector.tensor_copy(wt_picked[:], wt_tab[:].indirect(idx[:]))
         wt_sc = keep.tile([P, R], U8, align_bytes=64)
         nc.vector.tensor_copy(wt_sc[:].rearrange("p (t m) -> p m t", t=PACK), wt_plane[:].indirect(idx[:]))
-        wt_dealt = keep.tile([P, R], U16, align_bytes=64)
-        nc.vector.tensor_copy(
-            wt_dealt[:].rearrange("p (t m) -> p t m", t=PACK), wt_picked[:].rearrange("p (m t) -> p t m", t=PACK)
-        )
+        by_slice = wt_picked[:].rearrange("p (m t) -> p t m", t=PACK)
+        wt_first = keep.tile([P, P], U16, align_bytes=64)
+        nc.vector.tensor_copy(wt_first[:], by_slice[:, 0, :])
         xt_picked = keep.tile([P, J], U32, align_bytes=64)
         nc.vector.tensor_copy(xt_picked[:], xt_tab[:].bitcast(U32).indirect(idx2[:]))
         xt_sc = keep.tile([P, J], U8, align_bytes=64)
-        nc.vector.tensor_copy(xt_sc[:], xt_plane[:].indirect(idx2[:]))
+        slots = J // 2
+        for s in range(2):
+            entries = idx2[:, s * slots // 16 : (s + 1) * slots // 16]
+            nc.vector.tensor_copy(xt_sc[:, s * slots : (s + 1) * slots], xt_plane[:].indirect(entries))
+        wt_rest = keep.tile([P, PACK - 1, P], U16, align_bytes=64, tag="xt_plane_then_dealt")
+        nc.vector.tensor_copy(wt_rest[:], by_slice[:, 1:, :])
 
-        a_psum = [psum.tile([P, J], F32, name=f"a_psum{t}") for t in range(PACK)]
-        for t in range(PACK):
+        def hidden(acc, t, cols):
             nc.tensor.matmul_mx(
-                out=a_psum[t][:],
-                lhsT=wt_dealt[:, t * P : (t + 1) * P].bitcast(E2M1X4),
+                out=acc,
+                lhsT=(wt_first[:] if t == 0 else wt_rest[:, t - 1, :]).bitcast(E2M1X4),
                 lhsT_scale=wt_sc[:, t * P : (t + 1) * P],
-                rhs=xt_picked[:].bitcast(E5M2X4),
-                rhs_scale=xt_sc[:],
+                rhs=xt_picked[:, cols].bitcast(E5M2X4),
+                rhs_scale=xt_sc[:, cols],
                 start=True,
                 stop=True,
             )
 
-        a = keep.tile([P, PACK, J], F32)
-        for t in range(PACK):
-            copy_on(nc, "V" if t == 0 else "S", a[:, t, :], a_psum[t][:])
+        a_first = keep.tile([P, J], F32)
+        for s in range(2):
+            cols = slice(s * slots, (s + 1) * slots)
+            bank = psum.tile([P, slots], F32, name=f"a_first_bank{s}")
+            hidden(bank[:], 0, cols)
+            copy_on(nc, "SV"[s], a_first[:, cols], bank[:])
+        bank_second = psum.tile([P, J], F32)
+        hidden(bank_second[:], 1, slice(0, J))
+        bank_last = psum.tile([P, 2, J], F32)
+        for t in (2, 3):
+            hidden(bank_last[:, t - 2, :], t, slice(0, J))
+        a = {0: a_first[:]}
 
         based = [keep.tile([P, C], F32, name=f"based{t}") for t in range(PACK)]
         diff = [keep.tile([P, C], F32, name=f"diff{t}", tag=f"diff{t}") for t in range(PACK)]
@@ -121,10 +133,10 @@ def tile_list_stamplead_chosen_one_postedout_kernel(
         hid = keep.tile([P, O, PACK], BF16, align_bytes=64)
 
         def fetch_base(t):
-            nc.scalar.activation(based[t][:], tb_tab[t][:].indirect(idx4[:]), ACT.Copy, scale=a[:, t, 0:1])
+            nc.scalar.activation(based[t][:], tb_tab[t][:].indirect(idx4[:]), ACT.Copy, scale=a[t][:, 0:1])
 
         def put(t, engine):
-            copy_on(nc, engine, pw[t][:].indirect(idx3[:]), a[:, t, :])
+            copy_on(nc, engine, pw[t][:].indirect(idx3[:]), a[t])
 
         def subtract(t, engine):
             engine.tensor_tensor(diff[t][:], pw[t][:], based[t][:], ALU.subtract)
@@ -132,35 +144,45 @@ def tile_list_stamplead_chosen_one_postedout_kernel(
         def magnitude(t):
             nc.scalar.activation(pg[t], diff[t][:], ACT.Abs)
 
-        def pick(t, engine):
-            copy_on(nc, engine, picked[:, t, :], pg[t].indirect(idx5[:]))
+        def pick(t, engine, s=None):
+            cols = slice(0, O) if s is None else slice(s * O // 2, (s + 1) * O // 2)
+            entries = idx5[:, cols.start // 16 : cols.stop // 16]
+            copy_on(nc, engine, picked[:, t, cols], pg[t].indirect(entries))
 
-        def weave(ts, cols):
-            nc.vector.tensor_copy(hid[:, cols, ts], picked[:, ts, cols].rearrange("p t o -> p o t"))
+        def weave(cols):
+            nc.vector.tensor_copy(
+                hid[:, cols, :].rearrange("p (c i) t -> p c t i", i=4),
+                picked[:, :, cols].rearrange("p t (c i) -> p c t i", i=4),
+            )
 
-        for t in range(PACK):
+        fetch_base(0)
+        a_rest = keep.tile([P, PACK - 1, J], F32, tag="tb0")
+        copy_on(nc, "S", a_rest[:, 0, :], bank_second[:])
+        copy_on(nc, "S", a_rest[:, 1:, :], bank_last[:])
+        for t in range(1, PACK):
+            a[t] = a_rest[:, t - 1, :]
             fetch_base(t)
+        for t in range(PACK):
             put(t, "V")
             subtract(t, nc.vector if t == 3 else nc.gpsimd)
-        pg_front = keep.tile([P, 3, C], F32, tag="tb_last_then_pg")
+        pg_front = keep.tile([P, 3, C], F32, tag="tb3")
         for t in range(3):
             pg[t] = pg_front[:, t, :]
-        magnitude(0)
-        magnitude(1)
+        for t in range(3):
+            magnitude(t)
         pick(0, "S")
-        magnitude(2)
         pg_last = keep.tile([P, C], F32, tag="diff2")
         pg[3] = pg_last[:]
         magnitude(3)
-        pick(3, "S")
         pick(1, "V")
         pick(2, "V")
-        weave(slice(0, 2), slice(0, O))
+        pick(3, "V", 0)
+        pick(3, "S", 1)
         places = O // 2
         p_rows = [keep.tile([P, O], F32, name=f"p_rows{h}") for h in range(HALVES)]
         ends = [keep.tile([P, U], F32, name=f"ends{h}") for h in range(HALVES)]
         for s in range(2):
-            weave(slice(2, 4), slice(s * places, (s + 1) * places))
+            weave(slice(s * places, (s + 1) * places))
         for s in range(2):
             cols = slice(s * places, (s + 1) * places)
             hid_codes = keep.tile([P, places], U32, name=f"hid_codes{s}", align_bytes=64)
@@ -179,7 +201,7 @@ def tile_list_stamplead_chosen_one_postedout_kernel(
                     start=True,
                     stop=True,
                 )
-                copy_on(nc, "V" if (s, h) == (1, 0) else "S", p_rows[h][:, cols], p_psum[:])
+                copy_on(nc, "SV"[s], p_rows[h][:, cols], p_psum[:])
         for h in range(HALVES):
             nc.scalar.activation(ends[h][:], p_rows[h][:].indirect(idx6[:]), ACT.Copy, scale=so_cols[:, h : h + 1])
         for h, queue in enumerate((nc.sync, nc.scalar)):

@@ -54,16 +54,13 @@ def tile_list_stamplead_chosen_one_postedout_kernel(
         wb_plane = keep.tile([P, N], U8, align_bytes=64)
         for plane in (wt_plane, xt_plane, wb_plane):
             nc.vector.memset(plane[:].bitcast(I32), 0)
-        pw = [keep.tile([P, C], F32, name=f"pw{t}") for t in range(PACK)]
-        page = [keep.tile([P, E], F32, name=f"page{h}") for h in range(HALVES)]
-        for tile in pw[:2]:
+        pw = [keep.tile([P, C], F32, name=f"pw{t}", tag=f"pw{t}") for t in range(PACK - 1)]
+        for tile in pw:
             nc.vector.memset(tile[:], 0.0)
-        for tile in pw[2:] + page:
-            nc.gpsimd.memset(tile[:], 0.0)
 
-        idx = load_list(nc, keep, offs, "idx")
-        wt_tab = keep.tile([P, V], U16, align_bytes=64)
+        wt_tab = keep.tile([P, V], U16, align_bytes=64, tag="wt_tab")
         nc.sync.dma_start(wt_tab[:].bitcast(I32), wt_words[0].bitcast(I32))
+        idx = load_list(nc, keep, offs, "idx")
         load_scale_rows(nc.sync, wt_plane, wt_scales)
         idx2 = load_list(nc, keep, offs2, "idx2")
         xt_tab = keep.tile([P, T], I32, align_bytes=64)
@@ -87,6 +84,9 @@ def tile_list_stamplead_chosen_one_postedout_kernel(
 
         wt_picked = keep.tile([P, R], U16, align_bytes=64)
         nc.vector.tensor_copy(wt_picked[:], wt_tab[:].indirect(idx[:]))
+        pw_last = keep.tile([P, C], F32, align_bytes=64, tag="wt_tab")
+        nc.gpsimd.memset(pw_last[:], 0.0)
+        pw.append(pw_last)
         wt_sc = keep.tile([P, R], U8, align_bytes=64)
         nc.vector.tensor_copy(wt_sc[:].rearrange("p (t m) -> p m t", t=PACK), wt_plane[:].indirect(idx[:]))
         by_slice = wt_picked[:].rearrange("p (m t) -> p t m", t=PACK)
@@ -129,6 +129,7 @@ def tile_list_stamplead_chosen_one_postedout_kernel(
         based = [keep.tile([P, C], F32, name=f"based{t}") for t in range(PACK)]
         diff = [keep.tile([P, C], F32, name=f"diff{t}", tag=f"diff{t}") for t in range(PACK)]
         pg = {}
+        page = []
         picked = keep.tile([P, PACK, O], F32)
         hid = keep.tile([P, O, PACK], BF16, align_bytes=64)
 
@@ -165,6 +166,10 @@ def tile_list_stamplead_chosen_one_postedout_kernel(
         for t in range(PACK):
             put(t, "V")
             subtract(t, nc.vector if t == 3 else nc.gpsimd)
+            if t in (0, 2):
+                tile = keep.tile([P, E], F32, name=f"page{t // 2}", tag=f"pw{t}")
+                nc.gpsimd.memset(tile[:], 0.0)
+                page.append(tile)
         pg_front = keep.tile([P, 3, C], F32, tag="tb3")
         for t in range(3):
             pg[t] = pg_front[:, t, :]

from contextlib import ExitStack

import concourse.mybir as mybir

K, T, J, R, V, C, X, O, N, U, E = 512, 1024, 256, 512, 1024, 512, 1024, 256, 256, 128, 512
FLOPS = 2 * K * R * J + 2 * R * N * O

F32 = mybir.dt.float32
BF16 = mybir.dt.bfloat16
I32 = mybir.dt.int32
U32 = mybir.dt.uint32
U16 = mybir.dt.uint16
U8 = mybir.dt.uint8
E4M3X4 = mybir.dt.float8_e4m3fn_x4
E5M2X4 = mybir.dt.float8_e5m2_x4
E2M1X4 = mybir.dt.float4_e2m1fn_x4
ACT = mybir.ActivationFunctionType
ALU = mybir.AluOpType

P = 128
PACK = 4
HALVES = N // P


def load_list(nc, pool, offs, name):
    tile = pool.tile(list(offs.shape), U16, name=name)
    nc.sync.dma_start(tile[:], offs)
    return tile


def load_scale_rows(queue, plane, scales):
    for q in range(4):
        queue.dma_start(plane[32 * q : 32 * q + 4, :].bitcast(I32), scales[0, 4 * q : 4 * q + 4, :].bitcast(I32))


def copy_on(nc, engine, out, in_):
    if engine == "V":
        nc.vector.tensor_copy(out, in_)
    else:
        nc.scalar.activation(out, in_, ACT.Copy)


def tile_list_stamplead_chosen_one_postedout_kernel(
    tc, xt_words, xt_scales, wt_words, wt_scales, tb, wb_words, wb_scales, so,
    offs, offs2, offs3, offs4, offs5, offs6, offs7, out,
):
    nc = tc.nc
    with ExitStack() as ctx:
        keep = ctx.enter_context(tc.tile_pool(name="keep", bufs=1))
        psum = ctx.enter_context(tc.psum_pool(name="psum", bufs=1))

        wt_plane = keep.tile([P, V], U8, align_bytes=64)
        xt_plane = keep.tile([P, T], U8, align_bytes=64, tag="xt_plane_then_dealt")
        wb_plane = keep.tile([P, N], U8, align_bytes=64)
        for plane in (wt_plane, xt_plane, wb_plane):
            nc.vector.memset(plane[:].bitcast(I32), 0)
        pw = [keep.tile([P, C], F32, name=f"pw{t}", tag=f"pw{t}") for t in range(PACK - 1)]
        for tile in pw:
            nc.vector.memset(tile[:], 0.0)

        wt_tab = keep.tile([P, V], U16, align_bytes=64, tag="wt_tab")
        nc.sync.dma_start(wt_tab[:].bitcast(I32), wt_words[0].bitcast(I32))
        idx = load_list(nc, keep, offs, "idx")
        load_scale_rows(nc.sync, wt_plane, wt_scales)
        idx2 = load_list(nc, keep, offs2, "idx2")
        xt_tab = keep.tile([P, T], I32, align_bytes=64)
        nc.sync.dma_start(xt_tab[:], xt_words[0].rearrange("p c r -> p (c r)").bitcast(I32))
        load_scale_rows(nc.sync, xt_plane, xt_scales)
        idx4 = load_list(nc, keep, offs4, "idx4")
        idx3 = load_list(nc, keep, offs3, "idx3")
        tb_rows = tb.rearrange("(p t) x -> t p x", t=PACK)
        tb_tab = [keep.tile([P, X], F32, name=f"tb{t}", tag=f"tb{t}") for t in range(PACK)]
        for t in range(PACK):
            nc.sync.dma_start(tb_tab[t][:], tb_rows[t])
        idx5 = load_list(nc, keep, offs5, "idx5")
        wb_codes = keep.tile([P, 2 * N], U8, align_bytes=64)
        nc.sync.dma_start(wb_codes[:].bitcast(I32), wb_words[0].bitcast(I32))
        load_scale_rows(nc.sync, wb_plane, wb_scales)
        idx6 = load_list(nc, keep, offs6, "idx6")
        idx7 = load_list(nc, keep, offs7, "idx7")
        so_cols = keep.tile([P, HALVES], F32)
        with nc.allow_non_contiguous_dma(reason="one weight a partition for each half of the output features"):
            nc.sync.dma_start(so_cols[:], so.rearrange("(h p) o -> p (h o)", p=P))

        wt_picked = keep.tile([P, R], U16, align_bytes=64)
        nc.vector.tensor_copy(wt_picked[:], wt_tab[:].indirect(idx[:]))
        pw_last = keep.tile([P, C], F32, align_bytes=64, tag="wt_tab")
        nc.gpsimd.memset(pw_last[:], 0.0)
        pw.append(pw_last)
        wt_sc = keep.tile([P, R], U8, align_bytes=64)
        nc.vector.tensor_copy(wt_sc[:].rearrange("p (t m) -> p m t", t=PACK), wt_plane[:].indirect(idx[:]))
        by_slice = wt_picked[:].rearrange("p (m t) -> p t m", t=PACK)
        wt_first = keep.tile([P, P], U16, align_bytes=64)
        nc.vector.tensor_copy(wt_first[:], by_slice[:, 0, :])
        xt_picked = keep.tile([P, J], U32, align_bytes=64)
        nc.vector.tensor_copy(xt_picked[:], xt_tab[:].bitcast(U32).indirect(idx2[:]))
        xt_sc = keep.tile([P, J], U8, align_bytes=64)
        slots = J // 2
        for s in range(2):
            entries = idx2[:, s * slots // 16 : (s + 1) * slots // 16]
            nc.vector.tensor_copy(xt_sc[:, s * slots : (s + 1) * slots], xt_plane[:].indirect(entries))
        wt_rest = keep.tile([P, PACK - 1, P], U16, align_bytes=64, tag="xt_plane_then_dealt")
        nc.vector.tensor_copy(wt_rest[:], by_slice[:, 1:, :])

        def hidden(acc, t, cols):
            nc.tensor.matmul_mx(
                out=acc,
                lhsT=(wt_first[:] if t == 0 else wt_rest[:, t - 1, :]).bitcast(E2M1X4),
                lhsT_scale=wt_sc[:, t * P : (t + 1) * P],
                rhs=xt_picked[:, cols].bitcast(E5M2X4),
                rhs_scale=xt_sc[:, cols],
                start=True,
                stop=True,
            )

        a_first = keep.tile([P, J], F32)
        for s in range(2):
            cols = slice(s * slots, (s + 1) * slots)
            bank = psum.tile([P, slots], F32, name=f"a_first_bank{s}")
            hidden(bank[:], 0, cols)
            copy_on(nc, "SV"[s], a_first[:, cols], bank[:])
        bank_second = psum.tile([P, J], F32)
        hidden(bank_second[:], 1, slice(0, J))
        bank_last = psum.tile([P, 2, J], F32)
        for t in (2, 3):
            hidden(bank_last[:, t - 2, :], t, slice(0, J))
        a = {0: a_first[:]}

        based = [keep.tile([P, C], F32, name=f"based{t}") for t in range(PACK)]
        diff = [keep.tile([P, C], F32, name=f"diff{t}", tag=f"diff{t}") for t in range(PACK)]
        pg = {}
        page = []
        picked = keep.tile([P, PACK, O], F32)
        hid = keep.tile([P, O, PACK], BF16, align_bytes=64)

        def fetch_base(t):
            nc.scalar.activation(based[t][:], tb_tab[t][:].indirect(idx4[:]), ACT.Copy, scale=a[t][:, 0:1])

        def put(t, engine):
            copy_on(nc, engine, pw[t][:].indirect(idx3[:]), a[t])

        def subtract(t, engine):
            engine.tensor_tensor(diff[t][:], pw[t][:], based[t][:], ALU.subtract)

        def magnitude(t):
            nc.scalar.activation(pg[t], diff[t][:], ACT.Abs)

        def pick(t, engine, s=None):
            cols = slice(0, O) if s is None else slice(s * O // 2, (s + 1) * O // 2)
            entries = idx5[:, cols.start // 16 : cols.stop // 16]
            copy_on(nc, engine, picked[:, t, cols], pg[t].indirect(entries))

        def weave(cols):
            nc.vector.tensor_copy(
                hid[:, cols, :].rearrange("p (c i) t -> p c t i", i=4),
                picked[:, :, cols].rearrange("p t (c i) -> p c t i", i=4),
            )

        fetch_base(0)
        a_rest = keep.tile([P, PACK - 1, J], F32, tag="tb0")
        copy_on(nc, "S", a_rest[:, 0, :], bank_second[:])
        copy_on(nc, "S", a_rest[:, 1:, :], bank_last[:])
        for t in range(1, PACK):
            a[t] = a_rest[:, t - 1, :]
            fetch_base(t)
        for t in range(PACK):
            put(t, "V")
            subtract(t, nc.vector if t == 3 else nc.gpsimd)
            if t in (0, 2):
                tile = keep.tile([P, E], F32, name=f"page{t // 2}", tag=f"pw{t}")
                nc.gpsimd.memset(tile[:], 0.0)
                page.append(tile)
        pg_front = keep.tile([P, 3, C], F32, tag="tb3")
        for t in range(3):
            pg[t] = pg_front[:, t, :]
        for t in range(3):
            magnitude(t)
        pick(0, "S")
        pg_last = keep.tile([P, C], F32, tag="diff2")
        pg[3] = pg_last[:]
        magnitude(3)
        pick(1, "V")
        pick(2, "V")
        pick(3, "V", 0)
        pick(3, "S", 1)
        places = O // 2
        p_rows = [keep.tile([P, O], F32, name=f"p_rows{h}") for h in range(HALVES)]
        ends = [keep.tile([P, U], F32, name=f"ends{h}") for h in range(HALVES)]
        for s in range(2):
            weave(slice(s * places, (s + 1) * places))
        for s in range(2):
            cols = slice(s * places, (s + 1) * places)
            hid_codes = keep.tile([P, places], U32, name=f"hid_codes{s}", align_bytes=64)
            hid_sc = keep.tile([P, places], U8, name=f"hid_sc{s}", align_bytes=64)
            nc.vector.quantize_mx(
                out=hid_codes[:].bitcast(E4M3X4), scales=hid_sc[:], in_=hid[:, cols, :].rearrange("p o t -> p (o t)")
            )
            for h in range(HALVES):
                p_psum = psum.tile([P, places], F32, name=f"p_psum{s}{h}")
                nc.tensor.matmul_mx(
                    out=p_psum[:],
                    lhsT=wb_codes[:, 2 * h * P : 2 * (h + 1) * P].bitcast(E2M1X4),
                    lhsT_scale=wb_plane[:, h * P : (h + 1) * P],
                    rhs=hid_codes[:].bitcast(E4M3X4),
                    rhs_scale=hid_sc[:],
                    start=True,
                    stop=True,
                )
                copy_on(nc, "SV"[s], p_rows[h][:, cols], p_psum[:])
        for h in range(HALVES):
            nc.scalar.activation(ends[h][:], p_rows[h][:].indirect(idx6[:]), ACT.Copy, scale=so_cols[:, h : h + 1])
        for h, queue in enumerate((nc.sync, nc.scalar)):
            copy_on(nc, "VS"[h], page[h][:].indirect(idx7[:]), ends[h][:])
            queue.dma_start(out[h * P : (h + 1) * P, :], page[h][:])
